import numpy as np
import ml_dtypes


def mxq(x, axis, fmt="e4m3"):
    dtype, down = {"e4m3": (ml_dtypes.float8_e4m3fn, 7), "e5m2": (ml_dtypes.float8_e5m2, 14)}[fmt]
    v = np.moveaxis(np.asarray(x, np.float32).astype(ml_dtypes.bfloat16).astype(np.float64), axis, -1)
    blocks = v.reshape(v.shape[:-1] + (-1, 32))
    amax = np.abs(blocks).max(-1, keepdims=True)
    byte = np.maximum(np.where(amax > 0, np.frexp(amax)[1] - 1 + 127, 0) - down, 1)
    scale = np.exp2(byte - 127.0)
    codes = (blocks / scale).astype(np.float32).astype(dtype).astype(np.float64)
    return np.moveaxis((codes * scale).reshape(v.shape), -1, axis)


WIDE = False


def mx_kscale(k):
    if not WIDE:
        return np.ones(k)
    levels = np.array([10, -10, 5, -5, 0])
    if k % 512:
        return np.exp2(np.random.permutation(np.resize(levels, k // 32))).repeat(32)
    a = np.empty((k // 512, 16))
    for p in range(k // 512):
        a[p, :8] = np.random.permutation(np.resize(levels, 8))
        for g in range(8):
            far = levels[np.abs(levels - a[p, g]) >= 10]
            a[p, g + 8] = far[np.random.randint(len(far))]
    return np.exp2(a.ravel()).repeat(32)


def f64(x):
    return np.asarray(x).astype(np.float64)


def striped(idx):
    return np.tile(idx.reshape(-1, 16).T, (8, 1)).astype(np.uint16)


def unstriped(offs):
    return offs[:16].T.reshape(-1).astype(np.int64)

def planes(y):
    n, m = y.shape
    v = y.astype(np.float32).astype(ml_dtypes.bfloat16).astype(np.float64).reshape(n // 32, 32, m)
    top = np.abs(v).max(1)
    byte = np.clip(np.where(top > 0, np.frexp(top)[1] - 1 + 127 - 7, 1), 1, 254)
    codes = (v * np.exp2(127.0 - byte)[:, None, :]).reshape(n, m).astype(np.float32).astype(ml_dtypes.float8_e4m3fn).view(np.uint8)
    words = codes.reshape(n // 512, 128, 4, m).transpose(0, 1, 3, 2)
    return np.ascontiguousarray(words), np.ascontiguousarray(byte.astype(np.uint8).reshape(n // 512, 16, m))


K, T, S, D, H = 512, 1024, 512, 2, 512


def setup_inputs():
    n = np.random.standard_normal
    s = mx_kscale(K)[:, None]
    u = mx_kscale(H)
    return {
        "xT": (n((K, T)) * s).astype(np.float32),
        "w1": (n((K, H)) / np.sqrt(K) / s * u).astype(np.float32),
        "w2": (n((H, H)) / np.sqrt(H) / u[:, None]).astype(np.float32),
        "taps": (n((H, D)) / np.sqrt(D)).astype(np.float32),
        "offs": striped(np.random.permutation(T)[:S]),
    }


def reference(xT, w1, w2, taps, offs):
    xq = mxq(f64(xT)[:, unstriped(offs)], 0, "e4m3")
    h = mxq(f64(w1), 0, "e4m3").T @ xq
    z = f64(taps)[:, 0:1] * h + f64(taps)[:, 1:2] * (np.pad(h, ((0, 0), (1, 0)))[:, :S])
    out_0 = mxq(f64(w2), 0, "e4m3").T @ mxq(z, 0, "e4m3")
    return (out_0,) + planes(out_0)

@@ -1,0 +1,162 @@
+from contextlib import ExitStack
+
+import concourse.mybir as mybir
+
+K, T, S, H = 512, 1024, 512, 512
+FLOPS = 2 * K * H * S + 2 * H * H * S
+
+F32 = mybir.dt.float32
+BF16 = mybir.dt.bfloat16
+I32 = mybir.dt.int32
+U32 = mybir.dt.uint32
+U16 = mybir.dt.uint16
+U8 = mybir.dt.uint8
+FP8X4 = mybir.dt.float8_e4m3fn_x4
+COPY = mybir.ActivationFunctionType.Copy
+MULT = mybir.AluOpType.mult
+ADD = mybir.AluOpType.add
+
+P = 128
+PACK = 4
+HALF = S // 2
+QUARTER = S // 4
+LINE = 4
+
+
+def tile_picked_dconv_none_lo_kernel(tc, xT, w1, w2, taps, offs, out_0, out_1, out_2):
+    nc = tc.nc
+    with ExitStack() as ctx:
+        keep = ctx.enter_context(tc.tile_pool(name="keep", bufs=1))
+        psum = ctx.enter_context(tc.psum_pool(name="psum", bufs=1))
+
+        def sb(name, shape, dtype):
+            return keep.tile(shape, dtype, name=name, align_bytes=64)
+
+        offsets = keep.tile([P, S // 16], U16, name="offsets")
+        nc.sync.dma_start(offsets[:], offs)
+        x_rows = xT.rearrange("(p j) n -> p j n", j=PACK)
+        x_raw = [sb(f"x_raw{j}", [P, T], F32) for j in range(PACK)]
+        for j in range(PACK):
+            nc.sync.dma_start(x_raw[j][:], x_rows[:, j, :])
+        w_raw = {}
+        for name, w in (("w1", w1), ("w2", w2)):
+            rows = w.rearrange("(p j) c -> p j c", j=PACK)
+            for half in range(2):
+                w_raw[name, half] = sb(f"{name}_raw{half}", [P, PACK, H // 2], F32)
+                nc.sync.dma_start(w_raw[name, half][:], rows[:, :, half * (H // 2):(half + 1) * (H // 2)])
+            if name == "w1":
+                tap = sb("tap", [P, PACK, 2], F32)
+                nc.sync.dma_start(tap[:], taps.rearrange("(p t) d -> p t d", t=PACK))
+
+        warm = sb("warm", [P, 8], F32)
+        nc.gpsimd.memset(warm[:], 0.0)
+        nc.scalar.activation(warm[:, 1:2], warm[:, 0:1], COPY)
+        prev = sb("prev", [P, PACK, S + 8], F32)
+        nc.gpsimd.memset(prev[:, :, 0:1], 0.0)
+
+        def quantise(codes, scales, grouped, lo, n):
+            nc.vector.quantize_mx(
+                out=codes[:, lo:lo + n].bitcast(FP8X4),
+                scales=scales[:, lo:lo + n],
+                in_=grouped[:, PACK * lo:PACK * (lo + n)],
+            )
+
+        def weave(copy, grouped, planes, lo, n):
+            copy(
+                grouped[:, PACK * lo:PACK * (lo + n)].rearrange("p (c i t) -> p c t i", i=LINE, t=PACK),
+                planes.rearrange("p t (c i) -> p c t i", i=LINE),
+            )
+
+        def deal(copy, grouped, raw, half):
+            m = P // 2
+            copy(
+                grouped[:].rearrange("p (t m j) -> p m j t", t=PACK, j=PACK)[:, half * m:(half + 1) * m],
+                raw[:].rearrange("p j (m t) -> p m j t", t=PACK),
+            )
+
+        def operand(name):
+            return (sb(name + "_bf", [P, PACK * S], BF16), sb(name + "_codes", [P, S], U32), sb(name + "_scales", [P, S], U8))
+
+        x_bf, x_codes, x_scales = operand("x")
+        w1_bf, w1_codes, w1_scales = operand("w1")
+        w2_bf, w2_codes, w2_scales = operand("w2")
+        z_bf, z_codes, z_scales = operand("z")
+        y_bf, y_codes, y_scales = operand("y")
+
+        picked = sb("picked", [P, PACK, S], F32)
+        for j in range(PACK):
+            nc.vector.tensor_copy(picked[:, j, :], x_raw[j][:].indirect(offsets[:]))
+        for c in range(2):
+            weave(nc.vector.tensor_copy, x_bf, picked[:, :, c * HALF:(c + 1) * HALF], c * HALF, HALF)
+        for half in range(2):
+            deal(nc.scalar.copy, w1_bf, w_raw["w1", half], half)
+        for c in range(2):
+            quantise(x_codes, x_scales, x_bf, c * HALF, HALF)
+        for u in range(2):
+            quantise(w1_codes, w1_scales, w1_bf, u * 2 * P, 2 * P)
+
+        def product(bank, w_codes, w_scales, t, a_codes, a_scales, lo, n):
+            nc.tensor.matmul_mx(
+                out=bank,
+                lhsT=w_codes[:, t * P:(t + 1) * P].bitcast(FP8X4),
+                lhsT_scale=w_scales[:, t * P:(t + 1) * P],
+                rhs=a_codes[:, lo:lo + n].bitcast(FP8X4),
+                rhs_scale=a_scales[:, lo:lo + n],
+                start=True,
+                stop=True,
+            )
+
+        h_banks = [[psum.tile([P, 2, HALF], F32, name=f"h{c}{u}") for u in range(2)] for c in range(2)]
+        for c in range(2):
+            for t in range(PACK):
+                product(h_banks[c][t // 2][:, t % 2, :], w1_codes, w1_scales, t, x_codes, x_scales, c * HALF, HALF)
+
+        z_planes = sb("z_planes", [P, PACK, S], BF16)
+        y = sb("y", [P, PACK, S], F32)
+        y_banks = [psum.tile([P, PACK, QUARTER], F32, name=f"y{q}") for q in range(4)]
+        y_rows = out_0.rearrange("(p t) n -> p t n", t=PACK)
+        words = out_1.rearrange("z p c r -> p (z c r)").bitcast(I32)
+
+        def convolve(c):
+            lo = c * HALF
+            for u in range(2):
+                for t in (2 * u, 2 * u + 1):
+                    nc.scalar.activation(prev[:, t, lo + 1:lo + 1 + HALF], h_banks[c][u][:, t % 2, :], COPY, scale=tap[:, t, 1:2])
+                for t in (2 * u, 2 * u + 1):
+                    nc.vector.scalar_tensor_tensor(
+                        z_planes[:, t, lo:lo + HALF], h_banks[c][u][:, t % 2, :], tap[:, t, 0:1], prev[:, t, lo:lo + HALF], MULT, ADD
+                    )
+
+        def second(c):
+            lo = c * HALF
+            weave(nc.vector.tensor_copy, z_bf, z_planes[:, :, lo:lo + HALF], lo, HALF)
+            quantise(z_codes, z_scales, z_bf, lo, HALF)
+            for q in (2 * c, 2 * c + 1):
+                for t in range(PACK):
+                    product(y_banks[q][:, t, :], w2_codes, w2_scales, t, z_codes, z_scales, q * QUARTER, QUARTER)
+
+        def leave(c):
+            lo = c * HALF
+            for q in (2 * c, 2 * c + 1):
+                cols = slice(q * QUARTER, (q + 1) * QUARTER)
+                nc.scalar.copy(y[:, :, cols], y_banks[q][:])
+            nc.sync.dma_start(y_rows[:, :, lo:lo + HALF], y[:, :, lo:lo + HALF])
+            for q in (2 * c, 2 * c + 1):
+                cols = slice(q * QUARTER, (q + 1) * QUARTER)
+                weave(nc.vector.tensor_copy, y_bf, y[:, :, cols], q * QUARTER, QUARTER)
+            quantise(y_codes, y_scales, y_bf, lo, HALF)
+            nc.sync.dma_start(words[:, lo:lo + HALF], y_codes[:, lo:lo + HALF].bitcast(I32))
+
+        convolve(0)
+        deal(nc.vector.tensor_copy, w2_bf, w_raw["w2", 0], 0)
+        deal(nc.scalar.copy, w2_bf, w_raw["w2", 1], 1)
+        quantise(w2_codes, w2_scales, w2_bf, 0, H)
+        second(0)
+        convolve(1)
+        second(1)
+        leave(0)
+        leave(1)
+        scale_rows = out_2.rearrange("z q c -> (z q) c").bitcast(I32)
+        for quad in range(4):
+            queue = nc.scalar if quad % 2 else nc.sync
+            queue.dma_start(scale_rows[4 * quad:4 * quad + 4, :], y_scales[32 * quad:32 * quad + 4, :].bitcast(I32))

@@ -67,33 +67,41 @@ def tile_picked_dconv_none_lo_kernel(tc, xT, w1, w2, taps, offs, out_0, out_1, o
                 planes.rearrange("p t (c i) -> p c t i", i=LINE),
             )
 
-        def deal(copy, grouped, raw, half):
-            m = P // 2
+        def deal(copy, grouped, raw, half, a, b):
+            m = half * (P // 2)
             copy(
-                grouped[:].rearrange("p (t m j) -> p m j t", t=PACK, j=PACK)[:, half * m:(half + 1) * m],
-                raw[:].rearrange("p j (m t) -> p m j t", t=PACK),
+                grouped[:].rearrange("p (t m j) -> p m j t", t=PACK, j=PACK)[:, m + a:m + b],
+                raw[:].rearrange("p j (m t) -> p m j t", t=PACK)[:, a:b],
             )
 
         def operand(name):
             return (sb(name + "_bf", [P, PACK * S], BF16), sb(name + "_codes", [P, S], U32), sb(name + "_scales", [P, S], U8))
 
         x_bf, x_codes, x_scales = operand("x")
-        w1_bf, w1_codes, w1_scales = operand("w1")
-        w2_bf, w2_codes, w2_scales = operand("w2")
+        w_bf, w1_codes, w1_scales = operand("w1")
+        w2_codes, w2_scales = sb("w2_codes", [P, H], U32), sb("w2_scales", [P, H], U8)
         z_bf, z_codes, z_scales = operand("z")
         y_bf, y_codes, y_scales = operand("y")
 
         picked = sb("picked", [P, PACK, S], F32)
         for j in range(PACK):
             nc.vector.tensor_copy(picked[:, j, :], x_raw[j][:].indirect(offsets[:]))
+        def weave_pair(copy, first, lo, n):
+            copy(
+                x_bf[:, PACK * lo:PACK * (lo + n)].rearrange("p (c i t) -> p c t i", i=LINE, t=PACK)[:, :, first:first + 2, :],
+                picked[:, first:first + 2, lo:lo + n].rearrange("p t (c i) -> p c t i", i=LINE),
+            )
+
+        weave_pair(nc.scalar.copy, 0, 0, S)
         for c in range(2):
-            weave(nc.vector.tensor_copy, x_bf, picked[:, :, c * HALF:(c + 1) * HALF], c * HALF, HALF)
-        for half in range(2):
-            deal(nc.scalar.copy, w1_bf, w_raw["w1", half], half)
+            weave_pair(nc.vector.tensor_copy, 2, c * HALF, HALF)
+        deal(nc.scalar.copy, w_bf, w_raw["w1", 0], 0, 0, 64)
         for c in range(2):
             quantise(x_codes, x_scales, x_bf, c * HALF, HALF)
-        for u in range(2):
-            quantise(w1_codes, w1_scales, w1_bf, u * 2 * P, 2 * P)
+        deal(nc.scalar.copy, w_bf, w_raw["w1", 1], 1, 0, 40)
+        deal(nc.vector.tensor_copy, w_bf, w_raw["w1", 1], 1, 40, 64)
+        for t in range(PACK):
+            quantise(w1_codes, w1_scales, w_bf, t * P, P)
 
         def product(bank, w_codes, w_scales, t, a_codes, a_scales, lo, n):
             nc.tensor.matmul_mx(
@@ -106,56 +114,90 @@ def tile_picked_dconv_none_lo_kernel(tc, xT, w1, w2, taps, offs, out_0, out_1, o
                 stop=True,
             )
 
-        h_banks = [[psum.tile([P, 2, HALF], F32, name=f"h{c}{u}") for u in range(2)] for c in range(2)]
-        for c in range(2):
+        chunks = [256,256]
+        modes = "AB"
+        starts = [sum(chunks[:c]) for c in range(len(chunks))]
+        h_out = []
+        y_tags = []
+        bank = 0
+        for c, n in enumerate(chunks):
+            per = 1 if n > QUARTER else 2
+            tiles = [psum.tile([P, per, n], F32, name=f"h{c}{u}", tag=f"bank{bank + u}") for u in range(PACK // per)]
+            h_out.append([tiles[t // per][:, t % per, :] for t in range(PACK)])
+            y_tags.extend(f"bank{bank + u}" for u in range(n // QUARTER))
+            bank = bank + PACK // per
             for t in range(PACK):
-                product(h_banks[c][t // 2][:, t % 2, :], w1_codes, w1_scales, t, x_codes, x_scales, c * HALF, HALF)
+                product(h_out[c][t], w1_codes, w1_scales, t, x_codes, x_scales, starts[c], n)
 
         z_planes = sb("z_planes", [P, PACK, S], BF16)
+        cur = sb("cur", [P, PACK, S], F32)
         y = sb("y", [P, PACK, S], F32)
-        y_banks = [psum.tile([P, PACK, QUARTER], F32, name=f"y{q}") for q in range(4)]
+        y_banks = {}
         y_rows = out_0.rearrange("(p t) n -> p t n", t=PACK)
         words = out_1.rearrange("z p c r -> p (z c r)").bitcast(I32)
 
         def convolve(c):
-            lo = c * HALF
-            for u in range(2):
-                for t in (2 * u, 2 * u + 1):
-                    nc.scalar.activation(prev[:, t, lo + 1:lo + 1 + HALF], h_banks[c][u][:, t % 2, :], COPY, scale=tap[:, t, 1:2])
-                for t in (2 * u, 2 * u + 1):
-                    nc.vector.scalar_tensor_tensor(
-                        z_planes[:, t, lo:lo + HALF], h_banks[c][u][:, t % 2, :], tap[:, t, 0:1], prev[:, t, lo:lo + HALF], MULT, ADD
-                    )
+            lo, n = starts[c], chunks[c]
+            per = 1 if n > QUARTER else 2
+            for u in range(PACK // per):
+                for t in range(u * per, (u + 1) * per):
+                    nc.scalar.activation(prev[:, t, lo + 1:lo + 1 + n], h_out[c][t], COPY, scale=tap[:, t, 1:2])
+                    if modes[c] == "B":
+                        nc.scalar.activation(cur[:, t, lo:lo + n], h_out[c][t], COPY, scale=tap[:, t, 0:1])
+                if modes[c] != "B":
+                    for t in range(u * per, (u + 1) * per):
+                        nc.vector.scalar_tensor_tensor(
+                            z_planes[:, t, lo:lo + n], h_out[c][t], tap[:, t, 0:1], prev[:, t, lo:lo + n], MULT, ADD
+                        )
+
+        def z_weave(c):
+            lo, n = starts[c], chunks[c]
+            if modes[c] == "B":
+                nc.vector.tensor_tensor(
+                    z_bf[:, PACK * lo:PACK * (lo + n)].rearrange("p (c i t) -> p c t i", i=LINE, t=PACK),
+                    cur[:, :, lo:lo + n].rearrange("p t (c i) -> p c t i", i=LINE),
+                    prev[:, :, lo:lo + n].rearrange("p t (c i) -> p c t i", i=LINE),
+                    ADD,
+                )
+            else:
+                weave(nc.vector.tensor_copy if modes[c] == "A" else nc.scalar.copy, z_bf, z_planes[:, :, lo:lo + n], lo, n)
 
         def second(c):
-            lo = c * HALF
-            weave(nc.vector.tensor_copy, z_bf, z_planes[:, :, lo:lo + HALF], lo, HALF)
-            quantise(z_codes, z_scales, z_bf, lo, HALF)
-            for q in (2 * c, 2 * c + 1):
+            lo, n = starts[c], chunks[c]
+            quantise(z_codes, z_scales, z_bf, lo, n)
+            for q in range(lo // QUARTER, (lo + n) // QUARTER):
+                y_banks[q] = psum.tile([P, PACK, QUARTER], F32, name=f"y{q}", tag=y_tags[q])
                 for t in range(PACK):
                     product(y_banks[q][:, t, :], w2_codes, w2_scales, t, z_codes, z_scales, q * QUARTER, QUARTER)
 
-        def leave(c):
-            lo = c * HALF
-            for q in (2 * c, 2 * c + 1):
-                cols = slice(q * QUARTER, (q + 1) * QUARTER)
-                nc.scalar.copy(y[:, :, cols], y_banks[q][:])
-            nc.sync.dma_start(y_rows[:, :, lo:lo + HALF], y[:, :, lo:lo + HALF])
-            for q in (2 * c, 2 * c + 1):
-                cols = slice(q * QUARTER, (q + 1) * QUARTER)
-                weave(nc.vector.tensor_copy, y_bf, y[:, :, cols], q * QUARTER, QUARTER)
-            quantise(y_codes, y_scales, y_bf, lo, HALF)
-            nc.sync.dma_start(words[:, lo:lo + HALF], y_codes[:, lo:lo + HALF].bitcast(I32))
+        ymodes = "NNNN"
 
-        convolve(0)
-        deal(nc.vector.tensor_copy, w2_bf, w_raw["w2", 0], 0)
-        deal(nc.scalar.copy, w2_bf, w_raw["w2", 1], 1)
-        quantise(w2_codes, w2_scales, w2_bf, 0, H)
-        second(0)
-        convolve(1)
-        second(1)
-        leave(0)
-        leave(1)
+        def leave(q):
+            cols = slice(q * QUARTER, (q + 1) * QUARTER)
+            md = ymodes[q]
+            if md == "P":
+                weave(nc.vector.tensor_copy, y_bf, y_banks[q][:], q * QUARTER, QUARTER)
+            (nc.vector.tensor_copy if md == "V" else nc.scalar.copy)(y[:, :, cols], y_banks[q][:])
+            nc.sync.dma_start(y_rows[:, :, cols], y[:, :, cols])
+            if md == "S":
+                weave(nc.scalar.copy, y_bf, y_banks[q][:], q * QUARTER, QUARTER)
+            elif md != "P":
+                weave(nc.vector.tensor_copy, y_bf, y[:, :, cols], q * QUARTER, QUARTER)
+
+        def planes(q):
+            cols = slice(q * QUARTER, (q + 1) * QUARTER)
+            quantise(y_codes, y_scales, y_bf, q * QUARTER, QUARTER)
+            nc.sync.dma_start(words[:, cols], y_codes[:, cols].bitcast(I32))
+
+        def w2_deal(half):
+            deal(nc.vector.tensor_copy, w_bf, w_raw["w2", half], half, 0, 64)
+
+        def w2_quantise(u):
+            quantise(w2_codes, w2_scales, w_bf, u * 2 * P, 2 * P)
+
+        steps = {"c": convolve, "z": z_weave, "m": second, "y": leave, "q": planes, "w": w2_deal, "u": w2_quantise}
+        for step in "c0 w0 w1 u0 z0 u1 c1 m0 z1 m1 y0 q0 y1 q1 y2 q2 y3 q3".split():
+            steps[step[0]](int(step[1]))
         scale_rows = out_2.rearrange("z q c -> (z q) c").bitcast(I32)
         for quad in range(4):
             queue = nc.scalar if quad % 2 else nc.sync

@@ -33,16 +33,17 @@ def tile_picked_dconv_none_lo_kernel(tc, xT, w1, w2, taps, offs, out_0, out_1, o
             return keep.tile(shape, dtype, name=name, align_bytes=64)
 
         offsets = keep.tile([P, S // 16], U16, name="offsets")
-        nc.sync.dma_start(offsets[:], offs)
         x_rows = xT.rearrange("(p j) n -> p j n", j=PACK)
         x_raw = [sb(f"x_raw{j}", [P, T], F32) for j in range(PACK)]
         for j in range(PACK):
             nc.sync.dma_start(x_raw[j][:], x_rows[:, j, :])
+            if j == 0:
+                nc.sync.dma_start(offsets[:], offs)
         w_raw = {}
         for name, w in (("w1", w1), ("w2", w2)):
             rows = w.rearrange("(p j) c -> p j c", j=PACK)
             for half in range(2):
-                w_raw[name, half] = sb(f"{name}_raw{half}", [P, PACK, H // 2], F32)
+                w_raw[name, half] = keep.tile([P, PACK, H // 2], F32, name=f"{name}_raw{half}", tag=f"{name}_raw{half}", align_bytes=64)
                 nc.sync.dma_start(w_raw[name, half][:], rows[:, :, half * (H // 2):(half + 1) * (H // 2)])
             if name == "w1":
                 tap = sb("tap", [P, PACK, 2], F32)
@@ -85,23 +86,28 @@ def tile_picked_dconv_none_lo_kernel(tc, xT, w1, w2, taps, offs, out_0, out_1, o
 
         picked = sb("picked", [P, PACK, S], F32)
         for j in range(PACK):
-            nc.vector.tensor_copy(picked[:, j, :], x_raw[j][:].indirect(offsets[:]))
+            if j < PACK - 1:
+                nc.vector.tensor_copy(picked[:, j, :], x_raw[j][:].indirect(offsets[:]))
+            else:
+                for c in range(2):
+                    nc.vector.tensor_copy(picked[:, j, c * HALF:(c + 1) * HALF], x_raw[j][:].indirect(offsets[:, c * HALF // 16:(c + 1) * HALF // 16]))
         def weave_pair(copy, first, lo, n):
             copy(
                 x_bf[:, PACK * lo:PACK * (lo + n)].rearrange("p (c i t) -> p c t i", i=LINE, t=PACK)[:, :, first:first + 2, :],
                 picked[:, first:first + 2, lo:lo + n].rearrange("p t (c i) -> p c t i", i=LINE),
             )
 
-        weave_pair(nc.scalar.copy, 0, 0, S)
-        for c in range(2):
-            weave_pair(nc.vector.tensor_copy, 2, c * HALF, HALF)
+        weave_pair(nc.scalar.copy, 0, 0, HALF)
+        weave_pair(nc.vector.tensor_copy, 2, 0, HALF)
         deal(nc.scalar.copy, w_bf, w_raw["w1", 0], 0, 0, 64)
-        for c in range(2):
-            quantise(x_codes, x_scales, x_bf, c * HALF, HALF)
-        deal(nc.scalar.copy, w_bf, w_raw["w1", 1], 1, 0, 40)
-        deal(nc.vector.tensor_copy, w_bf, w_raw["w1", 1], 1, 40, 64)
+        quantise(x_codes, x_scales, x_bf, 0, HALF)
+        deal(nc.scalar.copy, w_bf, w_raw["w1", 1], 1, 0, 24)
+        deal(nc.vector.tensor_copy, w_bf, w_raw["w1", 1], 1, 24, 64)
         for t in range(PACK):
             quantise(w1_codes, w1_scales, w_bf, t * P, P)
+        x_late = keep.tile([P, PACK * HALF], BF16, name="x_late", tag="w1_raw1", align_bytes=64)
+        weave(nc.scalar.copy, x_late, picked[:, :, HALF:S], 0, HALF)
+        nc.vector.quantize_mx(out=x_codes[:, HALF:S].bitcast(FP8X4), scales=x_scales[:, HALF:S], in_=x_late[:])
 
         def product(bank, w_codes, w_scales, t, a_codes, a_scales, lo, n):
             nc.tensor.matmul_mx(
@@ -115,7 +121,7 @@ def tile_picked_dconv_none_lo_kernel(tc, xT, w1, w2, taps, offs, out_0, out_1, o
             )
 
         chunks = [256,256]
-        modes = "AB"
+        modes = "AA"
         starts = [sum(chunks[:c]) for c in range(len(chunks))]
         h_out = []
         y_tags = []
@@ -136,23 +142,29 @@ def tile_picked_dconv_none_lo_kernel(tc, xT, w1, w2, taps, offs, out_0, out_1, o
         y_rows = out_0.rearrange("(p t) n -> p t n", t=PACK)
         words = out_1.rearrange("z p c r -> p (z c r)").bitcast(I32)
 
-        def convolve(c):
-            lo, n = starts[c], chunks[c]
-            per = 1 if n > QUARTER else 2
-            for u in range(PACK // per):
-                for t in range(u * per, (u + 1) * per):
-                    nc.scalar.activation(prev[:, t, lo + 1:lo + 1 + n], h_out[c][t], COPY, scale=tap[:, t, 1:2])
-                    if modes[c] == "B":
-                        nc.scalar.activation(cur[:, t, lo:lo + n], h_out[c][t], COPY, scale=tap[:, t, 0:1])
-                if modes[c] != "B":
-                    for t in range(u * per, (u + 1) * per):
-                        nc.vector.scalar_tensor_tensor(
-                            z_planes[:, t, lo:lo + n], h_out[c][t], tap[:, t, 0:1], prev[:, t, lo:lo + n], MULT, ADD
-                        )
+        pieces = [[0,256,"A"],[256,128,"B"],[384,128,"B"]]
 
-        def z_weave(c):
-            lo, n = starts[c], chunks[c]
-            if modes[c] == "B":
+        def earlier(c):
+            lo = c * HALF
+            for t in range(PACK):
+                nc.scalar.activation(prev[:, t, lo + 1:lo + 1 + HALF], h_out[c][t], COPY, scale=tap[:, t, 1:2])
+                own = [(a, n) for a, n, md in pieces if md == "B" and a // HALF == c]
+                if own:
+                    a, n = own[0][0], sum(n for a, n in own)
+                    nc.scalar.activation(cur[:, t, a:a + n], h_out[c][t][:, a - lo:a - lo + n], COPY, scale=tap[:, t, 0:1])
+
+        def convolve(k):
+            a, n, md = pieces[k]
+            c = a // HALF
+            lo = c * HALF
+            for t in range(PACK):
+                nc.vector.scalar_tensor_tensor(
+                    z_planes[:, t, a:a + n], h_out[c][t][:, a - lo:a - lo + n], tap[:, t, 0:1], prev[:, t, a:a + n], MULT, ADD
+                )
+
+        def z_weave(k):
+            lo, n, md = pieces[k]
+            if md == "B":
                 nc.vector.tensor_tensor(
                     z_bf[:, PACK * lo:PACK * (lo + n)].rearrange("p (c i t) -> p c t i", i=LINE, t=PACK),
                     cur[:, :, lo:lo + n].rearrange("p t (c i) -> p c t i", i=LINE),
@@ -160,34 +172,38 @@ def tile_picked_dconv_none_lo_kernel(tc, xT, w1, w2, taps, offs, out_0, out_1, o
                     ADD,
                 )
             else:
-                weave(nc.vector.tensor_copy if modes[c] == "A" else nc.scalar.copy, z_bf, z_planes[:, :, lo:lo + n], lo, n)
+                weave(nc.vector.tensor_copy if md == "A" else nc.scalar.copy, z_bf, z_planes[:, :, lo:lo + n], lo, n)
 
-        def second(c):
-            lo, n = starts[c], chunks[c]
+        ymodes = "NNND"
+
+        def second(k):
+            lo, n, md = pieces[k]
             quantise(z_codes, z_scales, z_bf, lo, n)
             for q in range(lo // QUARTER, (lo + n) // QUARTER):
-                y_banks[q] = psum.tile([P, PACK, QUARTER], F32, name=f"y{q}", tag=y_tags[q])
+                per = 2 if ymodes[q] == "D" else PACK
+                y_banks[q] = [psum.tile([P, per, QUARTER], F32, name=f"y{q}{u}", tag=f"bank{q + u}") for u in range(PACK // per)]
                 for t in range(PACK):
-                    product(y_banks[q][:, t, :], w2_codes, w2_scales, t, z_codes, z_scales, q * QUARTER, QUARTER)
-
-        ymodes = "NNNN"
+                    product(y_banks[q][t // per][:, t % per, :], w2_codes, w2_scales, t, z_codes, z_scales, q * QUARTER, QUARTER)
 
         def leave(q):
             cols = slice(q * QUARTER, (q + 1) * QUARTER)
-            md = ymodes[q]
-            if md == "P":
-                weave(nc.vector.tensor_copy, y_bf, y_banks[q][:], q * QUARTER, QUARTER)
-            (nc.vector.tensor_copy if md == "V" else nc.scalar.copy)(y[:, :, cols], y_banks[q][:])
+            if ymodes[q] == "D":
+                nc.scalar.copy(y[:, 0:2, cols], y_banks[q][0][:])
+                nc.vector.tensor_copy(y[:, 2:4, cols], y_banks[q][1][:])
+            else:
+                nc.scalar.copy(y[:, :, cols], y_banks[q][0][:])
             nc.sync.dma_start(y_rows[:, :, cols], y[:, :, cols])
-            if md == "S":
-                weave(nc.scalar.copy, y_bf, y_banks[q][:], q * QUARTER, QUARTER)
-            elif md != "P":
+            if ymodes[q] == "S":
+                weave(nc.scalar.copy, y_bf, y_banks[q][0][:], q * QUARTER, QUARTER)
+            else:
                 weave(nc.vector.tensor_copy, y_bf, y[:, :, cols], q * QUARTER, QUARTER)
 
         def planes(q):
             cols = slice(q * QUARTER, (q + 1) * QUARTER)
             quantise(y_codes, y_scales, y_bf, q * QUARTER, QUARTER)
-            nc.sync.dma_start(words[:, cols], y_codes[:, cols].bitcast(I32))
+            if q >= 2:
+                cols = slice(0 if q == 2 else 3 * QUARTER, (q + 1) * QUARTER)
+                nc.sync.dma_start(words[:, cols], y_codes[:, cols].bitcast(I32))
 
         def w2_deal(half):
             deal(nc.vector.tensor_copy, w_bf, w_raw["w2", half], half, 0, 64)
@@ -195,8 +211,8 @@ def tile_picked_dconv_none_lo_kernel(tc, xT, w1, w2, taps, offs, out_0, out_1, o
         def w2_quantise(u):
             quantise(w2_codes, w2_scales, w_bf, u * 2 * P, 2 * P)
 
-        steps = {"c": convolve, "z": z_weave, "m": second, "y": leave, "q": planes, "w": w2_deal, "u": w2_quantise}
-        for step in "c0 w0 w1 u0 z0 u1 c1 m0 z1 m1 y0 q0 y1 q1 y2 q2 y3 q3".split():
+        steps = {"a": earlier, "c": convolve, "z": z_weave, "m": second, "y": leave, "q": planes, "w": w2_deal, "u": w2_quantise}
+        for step in "a0 w0 c0 w1 u0 z0 u1 a1 m0 z1 m1 z2 m2 y0 q0 y1 q1 y2 y3 q2 q3".split():
             steps[step[0]](int(step[1]))
         scale_rows = out_2.rearrange("z q c -> (z q) c").bitcast(I32)
         for quad in range(4):

from contextlib import ExitStack

import concourse.mybir as mybir

K, T, S, H = 512, 1024, 512, 512
FLOPS = 2 * K * H * S + 2 * H * H * S

F32 = mybir.dt.float32
BF16 = mybir.dt.bfloat16
I32 = mybir.dt.int32
U32 = mybir.dt.uint32
U16 = mybir.dt.uint16
U8 = mybir.dt.uint8
FP8X4 = mybir.dt.float8_e4m3fn_x4
COPY = mybir.ActivationFunctionType.Copy
MULT = mybir.AluOpType.mult
ADD = mybir.AluOpType.add

P = 128
PACK = 4
HALF = S // 2
QUARTER = S // 4
LINE = 4


def tile_picked_dconv_none_lo_kernel(tc, xT, w1, w2, taps, offs, out_0, out_1, out_2):
    nc = tc.nc
    with ExitStack() as ctx:
        keep = ctx.enter_context(tc.tile_pool(name="keep", bufs=1))
        psum = ctx.enter_context(tc.psum_pool(name="psum", bufs=1))

        def sb(name, shape, dtype):
            return keep.tile(shape, dtype, name=name, align_bytes=64)

        offsets = keep.tile([P, S // 16], U16, name="offsets")
        x_rows = xT.rearrange("(p j) n -> p j n", j=PACK)
        x_raw = [sb(f"x_raw{j}", [P, T], F32) for j in range(PACK)]
        for j in range(PACK):
            nc.sync.dma_start(x_raw[j][:], x_rows[:, j, :])
            if j == 0:
                nc.sync.dma_start(offsets[:], offs)
        w_raw = {}
        for name, w in (("w1", w1), ("w2", w2)):
            rows = w.rearrange("(p j) c -> p j c", j=PACK)
            for half in range(2):
                w_raw[name, half] = keep.tile([P, PACK, H // 2], F32, name=f"{name}_raw{half}", tag=f"{name}_raw{half}", align_bytes=64)
                nc.sync.dma_start(w_raw[name, half][:], rows[:, :, half * (H // 2):(half + 1) * (H // 2)])
            if name == "w1":
                tap = sb("tap", [P, PACK, 2], F32)
                nc.sync.dma_start(tap[:], taps.rearrange("(p t) d -> p t d", t=PACK))

        warm = sb("warm", [P, 8], F32)
        nc.gpsimd.memset(warm[:], 0.0)
        nc.scalar.activation(warm[:, 1:2], warm[:, 0:1], COPY)
        prev = sb("prev", [P, PACK, S + 8], F32)
        nc.gpsimd.memset(prev[:, :, 0:1], 0.0)

        def quantise(codes, scales, grouped, lo, n):
            nc.vector.quantize_mx(
                out=codes[:, lo:lo + n].bitcast(FP8X4),
                scales=scales[:, lo:lo + n],
                in_=grouped[:, PACK * lo:PACK * (lo + n)],
            )

        def weave(copy, grouped, planes, lo, n):
            copy(
                grouped[:, PACK * lo:PACK * (lo + n)].rearrange("p (c i t) -> p c t i", i=LINE, t=PACK),
                planes.rearrange("p t (c i) -> p c t i", i=LINE),
            )

        def deal(copy, grouped, raw, half, a, b):
            m = half * (P // 2)
            copy(
                grouped[:].rearrange("p (t m j) -> p m j t", t=PACK, j=PACK)[:, m + a:m + b],
                raw[:].rearrange("p j (m t) -> p m j t", t=PACK)[:, a:b],
            )

        def operand(name):
            return (sb(name + "_bf", [P, PACK * S], BF16), sb(name + "_codes", [P, S], U32), sb(name + "_scales", [P, S], U8))

        x_bf, x_codes, x_scales = operand("x")
        w_bf, w1_codes, w1_scales = operand("w1")
        w2_codes, w2_scales = sb("w2_codes", [P, H], U32), sb("w2_scales", [P, H], U8)
        z_bf, z_codes, z_scales = operand("z")
        y_bf, y_codes, y_scales = operand("y")

        picked = sb("picked", [P, PACK, S], F32)
        for j in range(PACK):
            if j < PACK - 1:
                nc.vector.tensor_copy(picked[:, j, :], x_raw[j][:].indirect(offsets[:]))
            else:
                for c in range(2):
                    nc.vector.tensor_copy(picked[:, j, c * HALF:(c + 1) * HALF], x_raw[j][:].indirect(offsets[:, c * HALF // 16:(c + 1) * HALF // 16]))
        def weave_pair(copy, first, lo, n):
            copy(
                x_bf[:, PACK * lo:PACK * (lo + n)].rearrange("p (c i t) -> p c t i", i=LINE, t=PACK)[:, :, first:first + 2, :],
                picked[:, first:first + 2, lo:lo + n].rearrange("p t (c i) -> p c t i", i=LINE),
            )

        weave_pair(nc.scalar.copy, 0, 0, HALF)
        weave_pair(nc.vector.tensor_copy, 2, 0, HALF)
        deal(nc.scalar.copy, w_bf, w_raw["w1", 0], 0, 0, 64)
        quantise(x_codes, x_scales, x_bf, 0, HALF)
        deal(nc.scalar.copy, w_bf, w_raw["w1", 1], 1, 0, 24)
        deal(nc.vector.tensor_copy, w_bf, w_raw["w1", 1], 1, 24, 64)
        for t in range(PACK):
            quantise(w1_codes, w1_scales, w_bf, t * P, P)
        x_late = keep.tile([P, PACK * HALF], BF16, name="x_late", tag="w1_raw1", align_bytes=64)
        weave(nc.scalar.copy, x_late, picked[:, :, HALF:S], 0, HALF)
        nc.vector.quantize_mx(out=x_codes[:, HALF:S].bitcast(FP8X4), scales=x_scales[:, HALF:S], in_=x_late[:])

        def product(bank, w_codes, w_scales, t, a_codes, a_scales, lo, n):
            nc.tensor.matmul_mx(
                out=bank,
                lhsT=w_codes[:, t * P:(t + 1) * P].bitcast(FP8X4),
                lhsT_scale=w_scales[:, t * P:(t + 1) * P],
                rhs=a_codes[:, lo:lo + n].bitcast(FP8X4),
                rhs_scale=a_scales[:, lo:lo + n],
                start=True,
                stop=True,
            )

        chunks = [256,256]
        modes = "AA"
        starts = [sum(chunks[:c]) for c in range(len(chunks))]
        h_out = []
        y_tags = []
        bank = 0
        for c, n in enumerate(chunks):
            per = 1 if n > QUARTER else 2
            tiles = [psum.tile([P, per, n], F32, name=f"h{c}{u}", tag=f"bank{bank + u}") for u in range(PACK // per)]
            h_out.append([tiles[t // per][:, t % per, :] for t in range(PACK)])
            y_tags.extend(f"bank{bank + u}" for u in range(n // QUARTER))
            bank = bank + PACK // per
            for t in range(PACK):
                product(h_out[c][t], w1_codes, w1_scales, t, x_codes, x_scales, starts[c], n)

        z_planes = sb("z_planes", [P, PACK, S], BF16)
        cur = sb("cur", [P, PACK, S], F32)
        y = sb("y", [P, PACK, S], F32)
        y_banks = {}
        y_rows = out_0.rearrange("(p t) n -> p t n", t=PACK)
        words = out_1.rearrange("z p c r -> p (z c r)").bitcast(I32)

        pieces = [[0,256,"A"],[256,128,"B"],[384,128,"B"]]

        def earlier(c):
            lo = c * HALF
            for t in range(PACK):
                nc.scalar.activation(prev[:, t, lo + 1:lo + 1 + HALF], h_out[c][t], COPY, scale=tap[:, t, 1:2])
                own = [(a, n) for a, n, md in pieces if md == "B" and a // HALF == c]
                if own:
                    a, n = own[0][0], sum(n for a, n in own)
                    nc.scalar.activation(cur[:, t, a:a + n], h_out[c][t][:, a - lo:a - lo + n], COPY, scale=tap[:, t, 0:1])

        def convolve(k):
            a, n, md = pieces[k]
            c = a // HALF
            lo = c * HALF
            for t in range(PACK):
                nc.vector.scalar_tensor_tensor(
                    z_planes[:, t, a:a + n], h_out[c][t][:, a - lo:a - lo + n], tap[:, t, 0:1], prev[:, t, a:a + n], MULT, ADD
                )

        def z_weave(k):
            lo, n, md = pieces[k]
            if md == "B":
                nc.vector.tensor_tensor(
                    z_bf[:, PACK * lo:PACK * (lo + n)].rearrange("p (c i t) -> p c t i", i=LINE, t=PACK),
                    cur[:, :, lo:lo + n].rearrange("p t (c i) -> p c t i", i=LINE),
                    prev[:, :, lo:lo + n].rearrange("p t (c i) -> p c t i", i=LINE),
                    ADD,
                )
            else:
                weave(nc.vector.tensor_copy if md == "A" else nc.scalar.copy, z_bf, z_planes[:, :, lo:lo + n], lo, n)

        ymodes = "NNND"

        def second(k):
            lo, n, md = pieces[k]
            quantise(z_codes, z_scales, z_bf, lo, n)
            for q in range(lo // QUARTER, (lo + n) // QUARTER):
                per = 2 if ymodes[q] == "D" else PACK
                y_banks[q] = [psum.tile([P, per, QUARTER], F32, name=f"y{q}{u}", tag=f"bank{q + u}") for u in range(PACK // per)]
                for t in range(PACK):
                    product(y_banks[q][t // per][:, t % per, :], w2_codes, w2_scales, t, z_codes, z_scales, q * QUARTER, QUARTER)

        def leave(q):
            cols = slice(q * QUARTER, (q + 1) * QUARTER)
            if ymodes[q] == "D":
                nc.scalar.copy(y[:, 0:2, cols], y_banks[q][0][:])
                nc.vector.tensor_copy(y[:, 2:4, cols], y_banks[q][1][:])
            else:
                nc.scalar.copy(y[:, :, cols], y_banks[q][0][:])
            nc.sync.dma_start(y_rows[:, :, cols], y[:, :, cols])
            if ymodes[q] == "S":
                weave(nc.scalar.copy, y_bf, y_banks[q][0][:], q * QUARTER, QUARTER)
            else:
                weave(nc.vector.tensor_copy, y_bf, y[:, :, cols], q * QUARTER, QUARTER)

        def planes(q):
            cols = slice(q * QUARTER, (q + 1) * QUARTER)
            quantise(y_codes, y_scales, y_bf, q * QUARTER, QUARTER)
            if q >= 2:
                cols = slice(0 if q == 2 else 3 * QUARTER, (q + 1) * QUARTER)
                nc.sync.dma_start(words[:, cols], y_codes[:, cols].bitcast(I32))

        def w2_deal(half):
            deal(nc.vector.tensor_copy, w_bf, w_raw["w2", half], half, 0, 64)

        def w2_quantise(u):
            quantise(w2_codes, w2_scales, w_bf, u * 2 * P, 2 * P)

        steps = {"a": earlier, "c": convolve, "z": z_weave, "m": second, "y": leave, "q": planes, "w": w2_deal, "u": w2_quantise}
        for step in "a0 w0 c0 w1 u0 z0 u1 a1 m0 z1 m1 z2 m2 y0 q0 y1 q1 y2 y3 q2 q3".split():
            steps[step[0]](int(step[1]))
        scale_rows = out_2.rearrange("z q c -> (z q) c").bitcast(I32)
        for quad in range(4):
            queue = nc.scalar if quad % 2 else nc.sync
            queue.dma_start(scale_rows[4 * quad:4 * quad + 4, :], y_scales[32 * quad:32 * quad + 4, :].bitcast(I32))
